import numpy as np
import ml_dtypes


def mxq(x, axis, fmt="e4m3"):
    dtype, down = {"e4m3": (ml_dtypes.float8_e4m3fn, 7), "e5m2": (ml_dtypes.float8_e5m2, 14)}[fmt]
    v = np.moveaxis(np.asarray(x, np.float32).astype(ml_dtypes.bfloat16).astype(np.float64), axis, -1)
    blocks = v.reshape(v.shape[:-1] + (-1, 32))
    amax = np.abs(blocks).max(-1, keepdims=True)
    byte = np.maximum(np.where(amax > 0, np.frexp(amax)[1] - 1 + 127, 0) - down, 1)
    scale = np.exp2(byte - 127.0)
    codes = (blocks / scale).astype(np.float32).astype(dtype).astype(np.float64)
    return np.moveaxis((codes * scale).reshape(v.shape), -1, axis)


WIDE = False


def mx_kscale(k):
    if not WIDE:
        return np.ones(k)
    levels = np.array([10, -10, 5, -5, 0])
    if k % 512:
        return np.exp2(np.random.permutation(np.resize(levels, k // 32))).repeat(32)
    a = np.empty((k // 512, 16))
    for p in range(k // 512):
        a[p, :8] = np.random.permutation(np.resize(levels, 8))
        for g in range(8):
            far = levels[np.abs(levels - a[p, g]) >= 10]
            a[p, g + 8] = far[np.random.randint(len(far))]
    return np.exp2(a.ravel()).repeat(32)


def f64(x):
    return np.asarray(x).astype(np.float64)


def striped(idx):
    return np.tile(idx.reshape(-1, 16).T, (8, 1)).astype(np.uint16)


def unstriped(offs):
    return offs[:16].T.reshape(-1).astype(np.int64)


def pack_weight(w):
    k, n = w.shape
    w = f64(np.asarray(w, np.float32).astype(ml_dtypes.bfloat16)).reshape(k // 32, 32, n)
    amax = np.abs(w).max(1)
    byte = np.clip(np.where(amax > 0, np.frexp(amax)[1] - 1 + 127 - 7, 1), 1, 254)
    scaled = (w * np.exp2(127.0 - byte)[:, None, :]).reshape(k, n).astype(np.float32)
    words = np.ascontiguousarray(scaled.reshape(k // 512, 128, 4, n).transpose(0, 1, 3, 2)).astype(ml_dtypes.float8_e4m3fn).view(np.uint8)
    return words, np.ascontiguousarray(byte.astype(np.uint8).reshape(k // 512, 16, n))


def unpack_weight(words, scales):
    g, p, n, _ = words.shape
    vals = np.ascontiguousarray(words).view(ml_dtypes.float8_e4m3fn).astype(np.float64) * np.repeat(np.exp2(scales.astype(np.float64) - 127.0), 8, axis=1)[..., None]
    return vals.transpose(0, 1, 3, 2).reshape(g * 512, n)


def sigmoid(v):
    return 1.0 / (1.0 + np.exp(-np.maximum(v, -700.0)))


K, T, S, V, W = 1024, 2048, 512, 256, 2048


def setup_inputs():
    n = np.random.standard_normal
    s = mx_kscale(K)[:, None]
    packed_xT = pack_weight(n((K, T)) * s)
    packed_eT = pack_weight(n((K, W)) * s)
    return {
        "x_words": packed_xT[0],
        "x_scales": packed_xT[1],
        "e_words": packed_eT[0],
        "e_scales": packed_eT[1],
        "wq": (n((K, V)) / np.sqrt(K) / s).astype(np.float32),
        "wb": (n((K, V)) / np.sqrt(K) / s).astype(np.float32),
        "act": (np.random.uniform(0.0, 1.0, (S, V)) ** 4).astype(np.float32),
        "disc": (np.random.uniform(0.8, 1.0, (S, 1))).astype(np.float32),
        "rew": (n((S, 1))).astype(np.float32),
        "offs": striped(np.random.permutation(T)[:S]),
        "now": striped(np.random.permutation(W)[:S]),
    }


def reference(x_words, x_scales, e_words, e_scales, wq, wb, act, disc, rew, offs, now):
    xq = unpack_weight(x_words, x_scales)[:, unstriped(offs)]
    wqq = mxq(f64(wq), 0, "e4m3")
    qv = xq.T @ wqq
    wbq = mxq(f64(wb), 0, "e4m3")
    be = sigmoid(xq.T @ wbq)
    top = qv.max(axis=1, keepdims=True)
    e_now = unpack_weight(e_words, e_scales)[:, unstriped(now)]
    q0 = e_now.T @ wqq
    return f64(act) * (f64(disc) * (qv - (be * qv) + be * top) + f64(rew) - q0)

@@ -1,0 +1,176 @@
+from contextlib import ExitStack
+
+import concourse.mybir as mybir
+from concourse.masks import make_identity
+
+K, T, S, V = 1024, 2048, 512, 256
+FLOPS = 3 * 2 * K * S * V
+
+F32 = mybir.dt.float32
+BF16 = mybir.dt.bfloat16
+I32 = mybir.dt.int32
+U32 = mybir.dt.uint32
+U16 = mybir.dt.uint16
+U8 = mybir.dt.uint8
+FP8X4 = mybir.dt.float8_e4m3fn_x4
+ALU = mybir.AluOpType
+ACT = mybir.ActivationFunctionType
+AX = mybir.AxisListType
+
+P = 128
+PACK = 4
+PASSES = K // (P * PACK)
+TILES = S // P
+HALF = S // 2
+
+
+def tile_picked_yoptc_td_p_kernel(
+    tc, x_words, x_scales, e_words, e_scales, wq, wb, act, disc, rew, offs, now, out
+):
+    nc = tc.nc
+    with ExitStack() as ctx:
+        keep = ctx.enter_context(tc.tile_pool(name="keep", bufs=1))
+        psum = ctx.enter_context(tc.psum_pool(name="psum", bufs=1))
+
+        offs_sb = keep.tile([P, S // 16], U16, name="offs_sb")
+        now_sb = keep.tile([P, S // 16], U16, name="now_sb")
+
+        ident = keep.tile([P, P], F32, name="ident")
+        make_identity(nc, ident[:])
+        xs_tab = keep.tile([P, T], U8, name="xs_tab", align_bytes=64)
+        es_tab = keep.tile([P, T], U8, name="es_tab", align_bytes=64)
+        rows = keep.tile([P, P], F32, name="rows")
+        nc.vector.memset(xs_tab[:].bitcast(I32), 0)
+        nc.vector.memset(es_tab[:].bitcast(I32), 0)
+        nc.vector.memset(rows[:], 0.0)
+        warm = keep.tile([P, 1], F32, name="warm")
+        warm2 = keep.tile([P, 1], F32, name="warm2")
+        nc.vector.memset(warm[:], 0.0)
+        nc.scalar.activation(out=warm2[:], in_=warm[:], func=ACT.Sigmoid)
+
+        def load_words(words, g, name):
+            tab = keep.tile([P, T], U32, name=name, align_bytes=64)
+            nc.sync.dma_start(out=tab[:].bitcast(I32), in_=words[g].rearrange("p n t -> p (n t)").bitcast(I32))
+            return tab
+
+        def load_w(w, g, name):
+            raw = keep.tile([P, PACK, V], F32, name=name)
+            nc.sync.dma_start(out=raw[:], in_=w[g * 512 : (g + 1) * 512, :].rearrange("(p j) n -> p j n", j=PACK))
+            return raw
+
+        x_tab = [None, None]
+        e_tab = [None, None]
+        x_tab[0] = load_words(x_words, 0, "x_tab0")
+        nc.sync.dma_start(offs_sb[:], offs)
+        wq_raw = [load_w(wq, g, "wq_raw%d" % g) for g in range(PASSES)]
+        x_tab[1] = load_words(x_words, 1, "x_tab1")
+        nc.sync.dma_start(now_sb[:], now)
+        wb_raw = [load_w(wb, g, "wb_raw%d" % g) for g in range(PASSES)]
+        e_tab[0] = load_words(e_words, 0, "e_tab0")
+        e_tab[1] = load_words(e_words, 1, "e_tab1")
+        act_sb = []
+        for h in range(2):
+            a = keep.tile([P, 2, V], F32, name="act%d" % h)
+            nc.sync.dma_start(out=a[:], in_=act[h * HALF : (h + 1) * HALF, :].rearrange("(j p) v -> p j v", p=P))
+            act_sb.append(a)
+
+        for tab, scales, k0 in ((xs_tab, x_scales, 0), (es_tab, e_scales, 8)):
+            for q in range(4):
+                nc.gpsimd.dma_start(
+                    out=tab[32 * q + k0 : 32 * q + k0 + 8, :].bitcast(I32),
+                    in_=scales[:, 4 * q : 4 * q + 4, :].bitcast(I32),
+                )
+        nc.gpsimd.dma_start(out=rows[0:TILES, :], in_=disc.rearrange("(j p) o -> j (p o)", p=P))
+        nc.gpsimd.dma_start(out=rows[TILES : 2 * TILES, :], in_=rew.rearrange("(j p) o -> j (p o)", p=P))
+        cols_ps = psum.tile([P, P], F32, name="cols_ps", tag="q0_bank3")
+        nc.tensor.transpose(cols_ps[:], rows[:], ident[:])
+        cols = keep.tile([P, 2 * TILES], F32, name="cols")
+        nc.scalar.copy(out=cols[:], in_=cols_ps[:, 0 : 2 * TILES])
+
+        def gather(tab, lst, lo, n, dt, name):
+            got = keep.tile([P, n], dt, name=name, align_bytes=64)
+            nc.vector.tensor_copy(got[:], tab[:].indirect(lst[:, lo // 16 : (lo + n) // 16]))
+            return got
+
+        def quantise(raws, name):
+            grouped = keep.tile([P, PASSES, V, PACK], BF16, name=name + "_bf", align_bytes=64)
+            for g in range(PASSES):
+                nc.scalar.copy(out=grouped[:, g], in_=raws[g][:].rearrange("p j n -> p n j"))
+            codes = keep.tile([P, PASSES * V], U32, name=name + "_codes", align_bytes=64)
+            planes = keep.tile([P, PASSES * V], U8, name=name + "_planes", align_bytes=64)
+            nc.vector.quantize_mx(
+                out=codes[:].bitcast(FP8X4), scales=planes[:], in_=grouped[:].rearrange("p g n j -> p (g n j)")
+            )
+            return codes, planes
+
+        def product(bank, words, bytes_, k0, w, j, g):
+            codes, planes = w
+            wt, lo = words
+            c = j * P - lo
+            nc.tensor.matmul_mx(
+                out=bank,
+                lhsT=wt[:, c : c + P].bitcast(FP8X4),
+                lhsT_scale=bytes_[k0 + 4 * g : P, j * P : (j + 1) * P],
+                rhs=codes[:, g * V : (g + 1) * V].bitcast(FP8X4),
+                rhs_scale=planes[:, g * V : (g + 1) * V],
+                start=(g == 0),
+                stop=(g == PASSES - 1),
+            )
+
+        x0 = gather(x_tab[0], offs_sb, 0, S, U32, "x0")
+        xs = gather(xs_tab, offs_sb, 0, S, U8, "xs")
+        wq_mx = quantise(wq_raw, "wq")
+        x1 = gather(x_tab[1], offs_sb, 0, S, U32, "x1")
+        es = gather(es_tab, now_sb, 0, S, U8, "es")
+
+        x_bank = [psum.tile([P, 2, V], F32, name="x_bank%d" % j) for j in range(TILES)]
+        top = keep.tile([P, TILES], F32, name="top")
+        base = keep.tile([P, TILES], F32, name="base")
+        for j in range(TILES):
+            product(x_bank[j][:, 0, :], (x0, 0), xs, 0, wq_mx, j, 0)
+            product(x_bank[j][:, 0, :], (x1, 0), xs, 0, wq_mx, j, 1)
+        for j in range(TILES):
+            nc.vector.tensor_reduce(out=top[:, j : j + 1], in_=x_bank[j][:, 0, :], axis=AX.X, op=ALU.max)
+            nc.scalar.activation(
+                out=base[:, j : j + 1], in_=top[:, j : j + 1], func=ACT.Identity,
+                scale=cols[:, j : j + 1], bias=cols[:, TILES + j : TILES + j + 1],
+            )
+        wb_mx = quantise(wb_raw, "wb")
+        e0 = gather(e_tab[0], now_sb, 0, S, U32, "e0")
+        stay = []
+        for j in range(TILES):
+            product(x_bank[j][:, 1, :], (x0, 0), xs, 0, wb_mx, j, 0)
+            product(x_bank[j][:, 1, :], (x1, 0), xs, 0, wb_mx, j, 1)
+            s = keep.tile([P, V], F32, name="s%d" % j)
+            nc.scalar.activation(out=s[:], in_=x_bank[j][:, 1, :], func=ACT.Sigmoid, scale=-1.0)
+            stay.append(s)
+        q0_bank = [psum.tile([P, V], F32, name="q0_bank%d" % j) for j in range(TILES)]
+        for j in range(TILES):
+            product(q0_bank[j][:], (e0, 0), es, 8, wq_mx, j, 0)
+        gap = []
+        for j in range(TILES):
+            d = keep.tile([P, V], F32, name="gap%d" % j)
+            nc.vector.scalar_tensor_tensor(
+                out=d[:], in0=x_bank[j][:, 0, :], scalar=top[:, j : j + 1], in1=stay[j][:],
+                op0=ALU.subtract, op1=ALU.mult,
+            )
+            gap.append(d)
+        e1 = [gather(e_tab[1], now_sb, h * HALF, HALF, U32, "e1_%d" % h) for h in range(2)]
+        for j in range(TILES):
+            product(q0_bank[j][:], (e1[j // 2], (j // 2) * HALF), es, 8, wq_mx, j, 1)
+        for h in range(2):
+            td = [keep.tile([P, V], F32, name="td%d" % (2 * h + i)) for i in range(2)]
+            for i in range(2):
+                j = 2 * h + i
+                nc.vector.scalar_tensor_tensor(
+                    out=td[i][:], in0=gap[j][:], scalar=cols[:, j : j + 1], in1=q0_bank[j][:],
+                    op0=ALU.mult, op1=ALU.subtract,
+                )
+            for i in range(2):
+                j = 2 * h + i
+                res = keep.tile([P, V], F32, name="res%d" % j)
+                nc.vector.scalar_tensor_tensor(
+                    out=res[:], in0=td[i][:], scalar=base[:, j : j + 1], in1=act_sb[h][:, i, :],
+                    op0=ALU.add, op1=ALU.mult,
+                )
+                nc.sync.dma_start(out=out[j * P : (j + 1) * P, :], in_=res[:])

@@ -58,13 +58,24 @@ def tile_picked_yoptc_td_p_kernel(
             nc.sync.dma_start(out=raw[:], in_=w[g * 512 : (g + 1) * 512, :].rearrange("(p j) n -> p j n", j=PACK))
             return raw
 
+        def load_scales(tab, scales, k0):
+            for q in range(4):
+                lo = 32 * q + k0
+                nc.sync.dma_start(
+                    out=tab[lo : lo + 8, :].bitcast(I32), in_=scales[:, 4 * q : 4 * q + 4, :].bitcast(I32)
+                )
+
         x_tab = [None, None]
         e_tab = [None, None]
         x_tab[0] = load_words(x_words, 0, "x_tab0")
         nc.sync.dma_start(offs_sb[:], offs)
+        load_scales(xs_tab, x_scales, 0)
         wq_raw = [load_w(wq, g, "wq_raw%d" % g) for g in range(PASSES)]
-        x_tab[1] = load_words(x_words, 1, "x_tab1")
         nc.sync.dma_start(now_sb[:], now)
+        load_scales(es_tab, e_scales, 8)
+        x_tab[1] = load_words(x_words, 1, "x_tab1")
+        nc.gpsimd.dma_start(out=rows[0:TILES, :], in_=disc.rearrange("(j p) o -> j (p o)", p=P))
+        nc.gpsimd.dma_start(out=rows[TILES : 2 * TILES, :], in_=rew.rearrange("(j p) o -> j (p o)", p=P))
         wb_raw = [load_w(wb, g, "wb_raw%d" % g) for g in range(PASSES)]
         e_tab[0] = load_words(e_words, 0, "e_tab0")
         e_tab[1] = load_words(e_words, 1, "e_tab1")
@@ -74,76 +85,69 @@ def tile_picked_yoptc_td_p_kernel(
             nc.sync.dma_start(out=a[:], in_=act[h * HALF : (h + 1) * HALF, :].rearrange("(j p) v -> p j v", p=P))
             act_sb.append(a)
 
-        for tab, scales, k0 in ((xs_tab, x_scales, 0), (es_tab, e_scales, 8)):
-            for q in range(4):
-                nc.gpsimd.dma_start(
-                    out=tab[32 * q + k0 : 32 * q + k0 + 8, :].bitcast(I32),
-                    in_=scales[:, 4 * q : 4 * q + 4, :].bitcast(I32),
-                )
-        nc.gpsimd.dma_start(out=rows[0:TILES, :], in_=disc.rearrange("(j p) o -> j (p o)", p=P))
-        nc.gpsimd.dma_start(out=rows[TILES : 2 * TILES, :], in_=rew.rearrange("(j p) o -> j (p o)", p=P))
-        cols_ps = psum.tile([P, P], F32, name="cols_ps", tag="q0_bank3")
-        nc.tensor.transpose(cols_ps[:], rows[:], ident[:])
-        cols = keep.tile([P, 2 * TILES], F32, name="cols")
-        nc.scalar.copy(out=cols[:], in_=cols_ps[:, 0 : 2 * TILES])
-
-        def gather(tab, lst, lo, n, dt, name):
-            got = keep.tile([P, n], dt, name=name, align_bytes=64)
+        def gather(tab, lst, lo, n, dt, name, tag=None):
+            got = keep.tile([P, n], dt, name=name, tag=tag or name, align_bytes=64)
             nc.vector.tensor_copy(got[:], tab[:].indirect(lst[:, lo // 16 : (lo + n) // 16]))
             return got
 
-        def quantise(raws, name):
-            grouped = keep.tile([P, PASSES, V, PACK], BF16, name=name + "_bf", align_bytes=64)
-            for g in range(PASSES):
-                nc.scalar.copy(out=grouped[:, g], in_=raws[g][:].rearrange("p j n -> p n j"))
-            codes = keep.tile([P, PASSES * V], U32, name=name + "_codes", align_bytes=64)
-            planes = keep.tile([P, PASSES * V], U8, name=name + "_planes", align_bytes=64)
+        def quantise(raw, name):
+            grouped = keep.tile([P, V, PACK], BF16, name=name + "_bf", align_bytes=64)
+            nc.scalar.copy(out=grouped[:], in_=raw[:].rearrange("p j n -> p n j"))
+            codes = keep.tile([P, V], U32, name=name + "_codes", align_bytes=64)
+            planes = keep.tile([P, V], U8, name=name + "_planes", align_bytes=64)
             nc.vector.quantize_mx(
-                out=codes[:].bitcast(FP8X4), scales=planes[:], in_=grouped[:].rearrange("p g n j -> p (g n j)")
+                out=codes[:].bitcast(FP8X4), scales=planes[:], in_=grouped[:].rearrange("p n j -> p (n j)")
             )
             return codes, planes
 
         def product(bank, words, bytes_, k0, w, j, g):
-            codes, planes = w
+            codes, planes = w[g]
             wt, lo = words
             c = j * P - lo
             nc.tensor.matmul_mx(
                 out=bank,
                 lhsT=wt[:, c : c + P].bitcast(FP8X4),
                 lhsT_scale=bytes_[k0 + 4 * g : P, j * P : (j + 1) * P],
-                rhs=codes[:, g * V : (g + 1) * V].bitcast(FP8X4),
-                rhs_scale=planes[:, g * V : (g + 1) * V],
+                rhs=codes[:].bitcast(FP8X4),
+                rhs_scale=planes[:],
                 start=(g == 0),
                 stop=(g == PASSES - 1),
             )
 
         x0 = gather(x_tab[0], offs_sb, 0, S, U32, "x0")
         xs = gather(xs_tab, offs_sb, 0, S, U8, "xs")
-        wq_mx = quantise(wq_raw, "wq")
-        x1 = gather(x_tab[1], offs_sb, 0, S, U32, "x1")
+        wq_mx = [quantise(wq_raw[g], "wq%d" % g) for g in range(PASSES)]
         es = gather(es_tab, now_sb, 0, S, U8, "es")
+        x1 = gather(x_tab[1], offs_sb, 0, S, U32, "x1", "es_tab")
 
         x_bank = [psum.tile([P, 2, V], F32, name="x_bank%d" % j) for j in range(TILES)]
         top = keep.tile([P, TILES], F32, name="top")
         base = keep.tile([P, TILES], F32, name="base")
         for j in range(TILES):
             product(x_bank[j][:, 0, :], (x0, 0), xs, 0, wq_mx, j, 0)
+        cols_ps = psum.tile([P, P], F32, name="cols_ps", tag="q0_bank3")
+        nc.tensor.transpose(cols_ps[:], rows[:], ident[:])
+        for j in range(TILES):
             product(x_bank[j][:, 0, :], (x1, 0), xs, 0, wq_mx, j, 1)
         for j in range(TILES):
             nc.vector.tensor_reduce(out=top[:, j : j + 1], in_=x_bank[j][:, 0, :], axis=AX.X, op=ALU.max)
+        wb_mx = [quantise(wb_raw[g], "wb%d" % g) for g in range(PASSES)]
+        cols = keep.tile([P, 2 * TILES], F32, name="cols", tag="wb_raw1")
+        nc.scalar.copy(out=cols[:], in_=cols_ps[:, 0 : 2 * TILES])
+        for j in range(TILES):
+            product(x_bank[j][:, 1, :], (x0, 0), xs, 0, wb_mx, j, 0)
+        stay = []
+        for j in range(TILES):
+            product(x_bank[j][:, 1, :], (x1, 0), xs, 0, wb_mx, j, 1)
+            s = keep.tile([P, V], F32, name="s%d" % j, align_bytes=64)
+            nc.scalar.activation(out=s[:], in_=x_bank[j][:, 1, :], func=ACT.Sigmoid, scale=-1.0)
+            stay.append(s)
+        for j in range(TILES):
             nc.scalar.activation(
                 out=base[:, j : j + 1], in_=top[:, j : j + 1], func=ACT.Identity,
                 scale=cols[:, j : j + 1], bias=cols[:, TILES + j : TILES + j + 1],
             )
-        wb_mx = quantise(wb_raw, "wb")
-        e0 = gather(e_tab[0], now_sb, 0, S, U32, "e0")
-        stay = []
-        for j in range(TILES):
-            product(x_bank[j][:, 1, :], (x0, 0), xs, 0, wb_mx, j, 0)
-            product(x_bank[j][:, 1, :], (x1, 0), xs, 0, wb_mx, j, 1)
-            s = keep.tile([P, V], F32, name="s%d" % j)
-            nc.scalar.activation(out=s[:], in_=x_bank[j][:, 1, :], func=ACT.Sigmoid, scale=-1.0)
-            stay.append(s)
+        e0 = gather(e_tab[0], now_sb, 0, S, U32, "e0", "wb1_bf")
         q0_bank = [psum.tile([P, V], F32, name="q0_bank%d" % j) for j in range(TILES)]
         for j in range(TILES):
             product(q0_bank[j][:], (e0, 0), es, 8, wq_mx, j, 0)
@@ -155,22 +159,29 @@ def tile_picked_yoptc_td_p_kernel(
                 op0=ALU.subtract, op1=ALU.mult,
             )
             gap.append(d)
-        e1 = [gather(e_tab[1], now_sb, h * HALF, HALF, U32, "e1_%d" % h) for h in range(2)]
+        e1 = [gather(e_tab[1], now_sb, h * HALF, HALF, U32, "e1_%d" % h, ("s3", None)[h]) for h in range(2)]
         for j in range(TILES):
             product(q0_bank[j][:], (e1[j // 2], (j // 2) * HALF), es, 8, wq_mx, j, 1)
-        for h in range(2):
-            td = [keep.tile([P, V], F32, name="td%d" % (2 * h + i)) for i in range(2)]
-            for i in range(2):
-                j = 2 * h + i
-                nc.vector.scalar_tensor_tensor(
-                    out=td[i][:], in0=gap[j][:], scalar=cols[:, j : j + 1], in1=q0_bank[j][:],
-                    op0=ALU.mult, op1=ALU.subtract,
-                )
-            for i in range(2):
-                j = 2 * h + i
-                res = keep.tile([P, V], F32, name="res%d" % j)
-                nc.vector.scalar_tensor_tensor(
-                    out=res[:], in0=td[i][:], scalar=base[:, j : j + 1], in1=act_sb[h][:, i, :],
-                    op0=ALU.add, op1=ALU.mult,
-                )
-                nc.sync.dma_start(out=out[j * P : (j + 1) * P, :], in_=res[:])
+        td = []
+
+        def subtract_q0(j):
+            t = keep.tile([P, V], F32, name="td%d" % j, tag=("e_tab1" if j == 0 else "td%d" % j), align_bytes=64)
+            nc.vector.scalar_tensor_tensor(
+                out=t[:], in0=gap[j][:], scalar=cols[:, j : j + 1], in1=q0_bank[j][:],
+                op0=ALU.mult, op1=ALU.subtract,
+            )
+            td.append(t)
+
+        def finish(j):
+            res = keep.tile([P, V], F32, name="res%d" % j)
+            nc.vector.scalar_tensor_tensor(
+                out=res[:], in0=td[j][:], scalar=base[:, j : j + 1], in1=act_sb[j // 2][:, j % 2, :],
+                op0=ALU.add, op1=ALU.mult,
+            )
+            nc.sync.dma_start(out=out[j * P : (j + 1) * P, :], in_=res[:])
+
+        for j in range(TILES + 1):
+            if j < TILES:
+                subtract_q0(j)
+            if j > 0:
+                finish(j - 1)

@@ -36,13 +36,13 @@ def tile_picked_yoptc_td_p_kernel(
         now_sb = keep.tile([P, S // 16], U16, name="now_sb")
 
         ident = keep.tile([P, P], F32, name="ident")
-        make_identity(nc, ident[:])
         xs_tab = keep.tile([P, T], U8, name="xs_tab", align_bytes=64)
         es_tab = keep.tile([P, T], U8, name="es_tab", align_bytes=64)
         rows = keep.tile([P, P], F32, name="rows")
-        nc.vector.memset(xs_tab[:].bitcast(I32), 0)
+        nc.gpsimd.memset(xs_tab[:].bitcast(I32), 0)
         nc.vector.memset(es_tab[:].bitcast(I32), 0)
         nc.vector.memset(rows[:], 0.0)
+        make_identity(nc, ident[:])
         warm = keep.tile([P, 1], F32, name="warm")
         warm2 = keep.tile([P, 1], F32, name="warm2")
         nc.vector.memset(warm[:], 0.0)
@@ -58,24 +58,25 @@ def tile_picked_yoptc_td_p_kernel(
             nc.sync.dma_start(out=raw[:], in_=w[g * 512 : (g + 1) * 512, :].rearrange("(p j) n -> p j n", j=PACK))
             return raw
 
-        def load_scales(tab, scales, k0):
-            for q in range(4):
-                lo = 32 * q + k0
+        def load_scales(tab, scales, quadrants):
+            for q in quadrants:
                 nc.sync.dma_start(
-                    out=tab[lo : lo + 8, :].bitcast(I32), in_=scales[:, 4 * q : 4 * q + 4, :].bitcast(I32)
+                    out=tab[32 * q : 32 * q + 8, :].bitcast(I32),
+                    in_=scales[:, 4 * q : 4 * q + 4, :].bitcast(I32),
                 )
 
         x_tab = [None, None]
         e_tab = [None, None]
-        x_tab[0] = load_words(x_words, 0, "x_tab0")
         nc.sync.dma_start(offs_sb[:], offs)
-        load_scales(xs_tab, x_scales, 0)
+        load_scales(xs_tab, x_scales, (2, 3, 0, 1))
+        load_scales(es_tab, e_scales, (2, 3))
+        x_tab[0] = load_words(x_words, 0, "x_tab0")
+        load_scales(es_tab, e_scales, (0, 1))
         wq_raw = [load_w(wq, g, "wq_raw%d" % g) for g in range(PASSES)]
         nc.sync.dma_start(now_sb[:], now)
-        load_scales(es_tab, e_scales, 8)
+        nc.sync.dma_start(out=rows[0:TILES, :], in_=disc.rearrange("(j p) o -> j (p o)", p=P))
+        nc.sync.dma_start(out=rows[TILES : 2 * TILES, :], in_=rew.rearrange("(j p) o -> j (p o)", p=P))
         x_tab[1] = load_words(x_words, 1, "x_tab1")
-        nc.gpsimd.dma_start(out=rows[0:TILES, :], in_=disc.rearrange("(j p) o -> j (p o)", p=P))
-        nc.gpsimd.dma_start(out=rows[TILES : 2 * TILES, :], in_=rew.rearrange("(j p) o -> j (p o)", p=P))
         wb_raw = [load_w(wb, g, "wb_raw%d" % g) for g in range(PASSES)]
         e_tab[0] = load_words(e_words, 0, "e_tab0")
         e_tab[1] = load_words(e_words, 1, "e_tab1")
@@ -114,11 +115,11 @@ def tile_picked_yoptc_td_p_kernel(
                 stop=(g == PASSES - 1),
             )
 
-        x0 = gather(x_tab[0], offs_sb, 0, S, U32, "x0")
         xs = gather(xs_tab, offs_sb, 0, S, U8, "xs")
+        x0 = gather(x_tab[0], offs_sb, 0, S, U32, "x0")
         wq_mx = [quantise(wq_raw[g], "wq%d" % g) for g in range(PASSES)]
-        es = gather(es_tab, now_sb, 0, S, U8, "es")
-        x1 = gather(x_tab[1], offs_sb, 0, S, U32, "x1", "es_tab")
+        es = gather(es_tab, now_sb, 0, S, U8, "es", "x_tab0")
+        x1 = [gather(x_tab[1], offs_sb, h * HALF, HALF, U32, "x1_%d" % h, ("es_tab", None)[h]) for h in range(2)]
 
         x_bank = [psum.tile([P, 2, V], F32, name="x_bank%d" % j) for j in range(TILES)]
         top = keep.tile([P, TILES], F32, name="top")
@@ -128,7 +129,7 @@ def tile_picked_yoptc_td_p_kernel(
         cols_ps = psum.tile([P, P], F32, name="cols_ps", tag="q0_bank3")
         nc.tensor.transpose(cols_ps[:], rows[:], ident[:])
         for j in range(TILES):
-            product(x_bank[j][:, 0, :], (x1, 0), xs, 0, wq_mx, j, 1)
+            product(x_bank[j][:, 0, :], (x1[j // 2], (j // 2) * HALF), xs, 0, wq_mx, j, 1)
         for j in range(TILES):
             nc.vector.tensor_reduce(out=top[:, j : j + 1], in_=x_bank[j][:, 0, :], axis=AX.X, op=ALU.max)
         wb_mx = [quantise(wb_raw[g], "wb%d" % g) for g in range(PASSES)]
@@ -138,7 +139,7 @@ def tile_picked_yoptc_td_p_kernel(
             product(x_bank[j][:, 1, :], (x0, 0), xs, 0, wb_mx, j, 0)
         stay = []
         for j in range(TILES):
-            product(x_bank[j][:, 1, :], (x1, 0), xs, 0, wb_mx, j, 1)
+            product(x_bank[j][:, 1, :], (x1[j // 2], (j // 2) * HALF), xs, 0, wb_mx, j, 1)
             s = keep.tile([P, V], F32, name="s%d" % j, align_bytes=64)
             nc.scalar.activation(out=s[:], in_=x_bank[j][:, 1, :], func=ACT.Sigmoid, scale=-1.0)
             stay.append(s)
@@ -150,18 +151,18 @@ def tile_picked_yoptc_td_p_kernel(
         e0 = gather(e_tab[0], now_sb, 0, S, U32, "e0", "wb1_bf")
         q0_bank = [psum.tile([P, V], F32, name="q0_bank%d" % j) for j in range(TILES)]
         for j in range(TILES):
-            product(q0_bank[j][:], (e0, 0), es, 8, wq_mx, j, 0)
+            product(q0_bank[j][:], (e0, 0), es, 0, wq_mx, j, 0)
         gap = []
         for j in range(TILES):
-            d = keep.tile([P, V], F32, name="gap%d" % j)
+            d = keep.tile([P, V], F32, name="gap%d" % j, tag=("e_tab0" if j == 0 else "gap%d" % j), align_bytes=64)
             nc.vector.scalar_tensor_tensor(
                 out=d[:], in0=x_bank[j][:, 0, :], scalar=top[:, j : j + 1], in1=stay[j][:],
                 op0=ALU.subtract, op1=ALU.mult,
             )
             gap.append(d)
-        e1 = [gather(e_tab[1], now_sb, h * HALF, HALF, U32, "e1_%d" % h, ("s3", None)[h]) for h in range(2)]
+        e1 = [gather(e_tab[1], now_sb, h * HALF, HALF, U32, "e1_%d" % h, "s%d" % (2 + h)) for h in range(2)]
         for j in range(TILES):
-            product(q0_bank[j][:], (e1[j // 2], (j // 2) * HALF), es, 8, wq_mx, j, 1)
+            product(q0_bank[j][:], (e1[j // 2], (j // 2) * HALF), es, 0, wq_mx, j, 1)
         td = []
 
         def subtract_q0(j):

from contextlib import ExitStack

import concourse.mybir as mybir
from concourse.masks import make_identity

K, T, S, V = 1024, 2048, 512, 256
FLOPS = 3 * 2 * K * S * V

F32 = mybir.dt.float32
BF16 = mybir.dt.bfloat16
I32 = mybir.dt.int32
U32 = mybir.dt.uint32
U16 = mybir.dt.uint16
U8 = mybir.dt.uint8
FP8X4 = mybir.dt.float8_e4m3fn_x4
ALU = mybir.AluOpType
ACT = mybir.ActivationFunctionType
AX = mybir.AxisListType

P = 128
PACK = 4
PASSES = K // (P * PACK)
TILES = S // P
HALF = S // 2


def tile_picked_yoptc_td_p_kernel(
    tc, x_words, x_scales, e_words, e_scales, wq, wb, act, disc, rew, offs, now, out
):
    nc = tc.nc
    with ExitStack() as ctx:
        keep = ctx.enter_context(tc.tile_pool(name="keep", bufs=1))
        psum = ctx.enter_context(tc.psum_pool(name="psum", bufs=1))

        offs_sb = keep.tile([P, S // 16], U16, name="offs_sb")
        now_sb = keep.tile([P, S // 16], U16, name="now_sb")

        ident = keep.tile([P, P], F32, name="ident")
        xs_tab = keep.tile([P, T], U8, name="xs_tab", align_bytes=64)
        es_tab = keep.tile([P, T], U8, name="es_tab", align_bytes=64)
        rows = keep.tile([P, P], F32, name="rows")
        nc.gpsimd.memset(xs_tab[:].bitcast(I32), 0)
        nc.vector.memset(es_tab[:].bitcast(I32), 0)
        nc.vector.memset(rows[:], 0.0)
        make_identity(nc, ident[:])
        warm = keep.tile([P, 1], F32, name="warm")
        warm2 = keep.tile([P, 1], F32, name="warm2")
        nc.vector.memset(warm[:], 0.0)
        nc.scalar.activation(out=warm2[:], in_=warm[:], func=ACT.Sigmoid)

        def load_words(words, g, name):
            tab = keep.tile([P, T], U32, name=name, align_bytes=64)
            nc.sync.dma_start(out=tab[:].bitcast(I32), in_=words[g].rearrange("p n t -> p (n t)").bitcast(I32))
            return tab

        def load_w(w, g, name):
            raw = keep.tile([P, PACK, V], F32, name=name)
            nc.sync.dma_start(out=raw[:], in_=w[g * 512 : (g + 1) * 512, :].rearrange("(p j) n -> p j n", j=PACK))
            return raw

        def load_scales(tab, scales, quadrants):
            for q in quadrants:
                nc.sync.dma_start(
                    out=tab[32 * q : 32 * q + 8, :].bitcast(I32),
                    in_=scales[:, 4 * q : 4 * q + 4, :].bitcast(I32),
                )

        x_tab = [None, None]
        e_tab = [None, None]
        nc.sync.dma_start(offs_sb[:], offs)
        load_scales(xs_tab, x_scales, (2, 3, 0, 1))
        load_scales(es_tab, e_scales, (2, 3))
        x_tab[0] = load_words(x_words, 0, "x_tab0")
        load_scales(es_tab, e_scales, (0, 1))
        wq_raw = [load_w(wq, g, "wq_raw%d" % g) for g in range(PASSES)]
        nc.sync.dma_start(now_sb[:], now)
        nc.sync.dma_start(out=rows[0:TILES, :], in_=disc.rearrange("(j p) o -> j (p o)", p=P))
        nc.sync.dma_start(out=rows[TILES : 2 * TILES, :], in_=rew.rearrange("(j p) o -> j (p o)", p=P))
        x_tab[1] = load_words(x_words, 1, "x_tab1")
        wb_raw = [load_w(wb, g, "wb_raw%d" % g) for g in range(PASSES)]
        e_tab[0] = load_words(e_words, 0, "e_tab0")
        e_tab[1] = load_words(e_words, 1, "e_tab1")
        act_sb = []
        for h in range(2):
            a = keep.tile([P, 2, V], F32, name="act%d" % h)
            nc.sync.dma_start(out=a[:], in_=act[h * HALF : (h + 1) * HALF, :].rearrange("(j p) v -> p j v", p=P))
            act_sb.append(a)

        def gather(tab, lst, lo, n, dt, name, tag=None):
            got = keep.tile([P, n], dt, name=name, tag=tag or name, align_bytes=64)
            nc.vector.tensor_copy(got[:], tab[:].indirect(lst[:, lo // 16 : (lo + n) // 16]))
            return got

        def quantise(raw, name):
            grouped = keep.tile([P, V, PACK], BF16, name=name + "_bf", align_bytes=64)
            nc.scalar.copy(out=grouped[:], in_=raw[:].rearrange("p j n -> p n j"))
            codes = keep.tile([P, V], U32, name=name + "_codes", align_bytes=64)
            planes = keep.tile([P, V], U8, name=name + "_planes", align_bytes=64)
            nc.vector.quantize_mx(
                out=codes[:].bitcast(FP8X4), scales=planes[:], in_=grouped[:].rearrange("p n j -> p (n j)")
            )
            return codes, planes

        def product(bank, words, bytes_, k0, w, j, g):
            codes, planes = w[g]
            wt, lo = words
            c = j * P - lo
            nc.tensor.matmul_mx(
                out=bank,
                lhsT=wt[:, c : c + P].bitcast(FP8X4),
                lhsT_scale=bytes_[k0 + 4 * g : P, j * P : (j + 1) * P],
                rhs=codes[:].bitcast(FP8X4),
                rhs_scale=planes[:],
                start=(g == 0),
                stop=(g == PASSES - 1),
            )

        xs = gather(xs_tab, offs_sb, 0, S, U8, "xs")
        x0 = gather(x_tab[0], offs_sb, 0, S, U32, "x0")
        wq_mx = [quantise(wq_raw[g], "wq%d" % g) for g in range(PASSES)]
        es = gather(es_tab, now_sb, 0, S, U8, "es", "x_tab0")
        x1 = [gather(x_tab[1], offs_sb, h * HALF, HALF, U32, "x1_%d" % h, ("es_tab", None)[h]) for h in range(2)]

        x_bank = [psum.tile([P, 2, V], F32, name="x_bank%d" % j) for j in range(TILES)]
        top = keep.tile([P, TILES], F32, name="top")
        base = keep.tile([P, TILES], F32, name="base")
        for j in range(TILES):
            product(x_bank[j][:, 0, :], (x0, 0), xs, 0, wq_mx, j, 0)
        cols_ps = psum.tile([P, P], F32, name="cols_ps", tag="q0_bank3")
        nc.tensor.transpose(cols_ps[:], rows[:], ident[:])
        for j in range(TILES):
            product(x_bank[j][:, 0, :], (x1[j // 2], (j // 2) * HALF), xs, 0, wq_mx, j, 1)
        for j in range(TILES):
            nc.vector.tensor_reduce(out=top[:, j : j + 1], in_=x_bank[j][:, 0, :], axis=AX.X, op=ALU.max)
        wb_mx = [quantise(wb_raw[g], "wb%d" % g) for g in range(PASSES)]
        cols = keep.tile([P, 2 * TILES], F32, name="cols", tag="wb_raw1")
        nc.scalar.copy(out=cols[:], in_=cols_ps[:, 0 : 2 * TILES])
        for j in range(TILES):
            product(x_bank[j][:, 1, :], (x0, 0), xs, 0, wb_mx, j, 0)
        stay = []
        for j in range(TILES):
            product(x_bank[j][:, 1, :], (x1[j // 2], (j // 2) * HALF), xs, 0, wb_mx, j, 1)
            s = keep.tile([P, V], F32, name="s%d" % j, align_bytes=64)
            nc.scalar.activation(out=s[:], in_=x_bank[j][:, 1, :], func=ACT.Sigmoid, scale=-1.0)
            stay.append(s)
        for j in range(TILES):
            nc.scalar.activation(
                out=base[:, j : j + 1], in_=top[:, j : j + 1], func=ACT.Identity,
                scale=cols[:, j : j + 1], bias=cols[:, TILES + j : TILES + j + 1],
            )
        e0 = gather(e_tab[0], now_sb, 0, S, U32, "e0", "wb1_bf")
        q0_bank = [psum.tile([P, V], F32, name="q0_bank%d" % j) for j in range(TILES)]
        for j in range(TILES):
            product(q0_bank[j][:], (e0, 0), es, 0, wq_mx, j, 0)
        gap = []
        for j in range(TILES):
            d = keep.tile([P, V], F32, name="gap%d" % j, tag=("e_tab0" if j == 0 else "gap%d" % j), align_bytes=64)
            nc.vector.scalar_tensor_tensor(
                out=d[:], in0=x_bank[j][:, 0, :], scalar=top[:, j : j + 1], in1=stay[j][:],
                op0=ALU.subtract, op1=ALU.mult,
            )
            gap.append(d)
        e1 = [gather(e_tab[1], now_sb, h * HALF, HALF, U32, "e1_%d" % h, "s%d" % (2 + h)) for h in range(2)]
        for j in range(TILES):
            product(q0_bank[j][:], (e1[j // 2], (j // 2) * HALF), es, 0, wq_mx, j, 1)
        td = []

        def subtract_q0(j):
            t = keep.tile([P, V], F32, name="td%d" % j, tag=("e_tab1" if j == 0 else "td%d" % j), align_bytes=64)
            nc.vector.scalar_tensor_tensor(
                out=t[:], in0=gap[j][:], scalar=cols[:, j : j + 1], in1=q0_bank[j][:],
                op0=ALU.mult, op1=ALU.subtract,
            )
            td.append(t)

        def finish(j):
            res = keep.tile([P, V], F32, name="res%d" % j)
            nc.vector.scalar_tensor_tensor(
                out=res[:], in0=td[j][:], scalar=base[:, j : j + 1], in1=act_sb[j // 2][:, j % 2, :],
                op0=ALU.add, op1=ALU.mult,
            )
            nc.sync.dma_start(out=out[j * P : (j + 1) * P, :], in_=res[:])

        for j in range(TILES + 1):
            if j < TILES:
                subtract_q0(j)
            if j > 0:
                finish(j - 1)
